import numpy as np
import ml_dtypes


def mxq(x, axis, fmt="e4m3"):
    dtype, down = {"e4m3": (ml_dtypes.float8_e4m3fn, 7), "e5m2": (ml_dtypes.float8_e5m2, 14)}[fmt]
    v = np.moveaxis(np.asarray(x, np.float32).astype(ml_dtypes.bfloat16).astype(np.float64), axis, -1)
    blocks = v.reshape(v.shape[:-1] + (-1, 32))
    amax = np.abs(blocks).max(-1, keepdims=True)
    byte = np.maximum(np.where(amax > 0, np.frexp(amax)[1] - 1 + 127, 0) - down, 1)
    scale = np.exp2(byte - 127.0)
    codes = (blocks / scale).astype(np.float32).astype(dtype).astype(np.float64)
    return np.moveaxis((codes * scale).reshape(v.shape), -1, axis)


WIDE = False


def mx_kscale(k):
    if not WIDE:
        return np.ones(k)
    levels = np.array([10, -10, 5, -5, 0])
    if k % 512:
        return np.exp2(np.random.permutation(np.resize(levels, k // 32))).repeat(32)
    a = np.empty((k // 512, 16))
    for p in range(k // 512):
        a[p, :8] = np.random.permutation(np.resize(levels, 8))
        for g in range(8):
            far = levels[np.abs(levels - a[p, g]) >= 10]
            a[p, g + 8] = far[np.random.randint(len(far))]
    return np.exp2(a.ravel()).repeat(32)


def f64(x):
    return np.asarray(x).astype(np.float64)


def striped(idx):
    return np.tile(np.asarray(idx).reshape(-1, 16).T, (8, 1)).astype(np.uint16)


def unstriped(offs):
    return offs[:16].T.reshape(-1).astype(np.int64)


def gelu(v):
    return 0.5 * v * (1.0 + np.tanh(0.7978845608028654 * (v + 0.044715 * v ** 3)))


E, T, I, F, J = 512, 2048, 512, 512, 512


def setup_inputs():
    n = np.random.standard_normal
    idx = np.random.permutation(T)[:I]
    fi = mx_kscale(I)
    ff = mx_kscale(F)
    ti = np.ones(T)
    ti[idx] = fi
    return {
        "tok": (n((E, T)) / ti).astype(np.float32),
        "wa": (n((I, F)) * 1 / np.sqrt(I) * fi[:, None]).astype(np.float32),
        "gain": (np.random.uniform(0.5, 2.0, (F, 1)) * ff[:, None]).astype(np.float32),
        "wb": (n((F, J)) * 1 / np.sqrt(F) / ff[:, None]).astype(np.float32),
        "offs": striped(idx),
    }


def reference(tok, wa, gain, wb, offs):
    idx = unstriped(offs)
    xt = f64(tok)[:, idx].T
    waq = mxq(f64(wa), 0, "e4m3")
    xtq = mxq(xt, 0, "e4m3")
    z = waq.T @ xtq
    g = gelu(z) * f64(gain)
    wbq = mxq(f64(wb), 0, "e4m3")
    gq = mxq(g, 0, "e4m3")
    y = wbq.T @ gq
    return y

@@ -1,0 +1,178 @@
+from contextlib import ExitStack
+
+import concourse.mybir as mybir
+from concourse.masks import make_identity
+
+E, T, I, F, J = 512, 2048, 512, 512, 512
+FLOPS = 2 * I * F * E + 2 * F * J * E
+
+F32 = mybir.dt.float32
+BF16 = mybir.dt.bfloat16
+U32 = mybir.dt.uint32
+U16 = mybir.dt.uint16
+U8 = mybir.dt.uint8
+FP8X4 = mybir.dt.float8_e4m3fn_x4
+GELU = mybir.ActivationFunctionType.Gelu_apprx_tanh
+MULT = mybir.AluOpType.mult
+
+P = 128
+PACK = 4
+BLOCKS = E // P
+HALF = J // 2
+WA_SPLIT = 96
+WINDOW_BYTES = 4 * T
+WB_HALF_BYTES = 4 * PACK * HALF
+KIB = 1024
+
+
+def tile_attend_tokenmixer_kernel(tc, tok, wa, gain, wb, offs, out):
+    nc = tc.nc
+    with ExitStack() as ctx:
+        keep = ctx.enter_context(tc.tile_pool(name="keep", bufs=1))
+        arena = ctx.enter_context(tc.tile_pool(name="arena", bufs=1))
+        psum = ctx.enter_context(tc.psum_pool(name="psum", bufs=1))
+
+        window_at = [b * WINDOW_BYTES for b in range(BLOCKS)]
+        wb_raw_at = [BLOCKS * WINDOW_BYTES + h * WB_HALF_BYTES for h in range(2)]
+
+        def work_tile(name, shape, dtype, at=None):
+            if at is None:
+                return keep.tile(shape, dtype, name=name, align_bytes=64)
+            return arena.tile(shape, dtype, name=name, align_bytes=64, offset=at)
+
+        offsets = keep.tile([P, I // 16], U16, name="offsets")
+        wa_raw = keep.tile([P, PACK, F], F32, name="wa_raw")
+        gain_cols = keep.tile([P, PACK], F32, name="gain_cols")
+        windows = [work_tile("window%d" % b, [P, T], F32, window_at[b]) for b in range(BLOCKS)]
+        wb_raw = [work_tile("wb_raw%d" % h, [P, PACK, HALF], F32, wb_raw_at[h]) for h in range(2)]
+
+        nc.sync.dma_start(out=wa_raw[:], in_=wa.rearrange("(p s) f -> p s f", s=PACK))
+        nc.sync.dma_start(offsets[:], offs)
+        nc.sync.dma_start(out=gain_cols[:], in_=gain.rearrange("(p t) o -> p (t o)", t=PACK))
+        for b in range(BLOCKS):
+            nc.sync.dma_start(out=windows[b][:], in_=tok[b * P : (b + 1) * P, :])
+        wb_rows = wb.rearrange("(p t) j -> p t j", t=PACK)
+        for h in range(2):
+            nc.sync.dma_start(out=wb_raw[h][:], in_=wb_rows[:, :, h * HALF : (h + 1) * HALF])
+
+        ident = keep.tile([P, P], F32, name="ident")
+        make_identity(nc, ident[:])
+        warm = keep.tile([P, 1], F32, name="warm")
+        nc.scalar.activation(out=warm[:], in_=ident[:, 0:1], func=GELU)
+
+        gain_full = gain_cols[:].rearrange("p (o t) -> p o t", o=1).to_broadcast([P, P, PACK])
+
+        def quantize(name, values, at=None):
+            width = values.shape[1] // PACK
+            codes = work_tile(name + "_codes", [P, width], U32, at)
+            scales = work_tile(name + "_scales", [P, width], U8)
+            nc.vector.quantize_mx(out=codes[:].bitcast(FP8X4), scales=scales[:], in_=values[:])
+            return codes, scales
+
+        def product(dst, stationary, column, moving):
+            cols = slice(column, column + P)
+            nc.tensor.matmul_mx(
+                out=dst,
+                lhsT=stationary[0][:, cols].bitcast(FP8X4),
+                lhsT_scale=stationary[1][:, cols],
+                rhs=moving[0][:].bitcast(FP8X4),
+                rhs_scale=moving[1][:],
+                start=True,
+                stop=True,
+            )
+
+        def gather(b):
+            picked = work_tile("picked%d" % b, [P, I], BF16)
+            nc.vector.tensor_copy(picked[:], windows[b][:].indirect(offsets[:]))
+            words = picked[:].bitcast(F32)
+            turned = psum.tile([P, 2, P], F32, name="turned", tag="turned")
+            for u in range(2):
+                nc.tensor.transpose(turned[:, u, :], words[:, u : I // 2 : 2], ident[:])
+            return turned
+
+        def interleave_x(b, turned, at=None):
+            x_bf = work_tile("x_bf%d" % b, [P, PACK * P], BF16, at)
+            nc.scalar.copy(
+                out=x_bf[:].bitcast(F32).rearrange("p (e u) -> p e u", u=2),
+                in_=turned[:].rearrange("p u e -> p e u"),
+            )
+            return x_bf
+
+        def first_product(xq):
+            z = psum.tile([P, PACK, P], F32, name="z", bufs=2)
+            for t in range(PACK):
+                product(z[:, t, :], waq, t * P, xq)
+            return z
+
+        def activate(b, z, at=None):
+            act = work_tile("act%d" % b, [P, P, PACK], F32, at)
+            nc.scalar.activation(out=act[:], in_=z[:].rearrange("p t e -> p e t"), func=GELU)
+            return act
+
+        def apply_gain(b, act, at=None):
+            g_bf = work_tile("g_bf%d" % b, [P, PACK * P], BF16, at)
+            nc.vector.tensor_tensor(
+                out=g_bf[:].rearrange("p (e t) -> p e t", t=PACK), in0=act[:], in1=gain_full, op=MULT
+            )
+            return g_bf
+
+        def interleave_wb(h, copy):
+            wb_bf = work_tile("wb_bf%d" % h, [P, PACK * HALF], BF16)
+            copy(
+                out=wb_bf[:].rearrange("p (c i t) -> p c t i", i=PACK, t=PACK),
+                in_=wb_raw[h][:].rearrange("p t (c i) -> p c t i", i=PACK),
+            )
+            return wb_bf
+
+        wa_dealt = wa_raw[:].rearrange("p s (m t) -> p t m s", t=PACK)
+        wa_bf = work_tile("wa_bf", [P, PACK * F], BF16)
+        wa_bf_dealt = wa_bf[:].rearrange("p (t m s) -> p t m s", t=PACK, s=PACK)
+        nc.vector.tensor_copy(out=wa_bf_dealt[:, :, 0:WA_SPLIT, :], in_=wa_dealt[:, :, 0:WA_SPLIT, :])
+        nc.scalar.copy(out=wa_bf_dealt[:, :, WA_SPLIT:P, :], in_=wa_dealt[:, :, WA_SPLIT:P, :])
+        waq = quantize("wa", wa_bf)
+
+        x_bf0 = interleave_x(0, gather(0))
+
+        turned1 = gather(1)
+        z0 = first_product(quantize("x0", x_bf0, window_at[1]))
+        x_bf1 = interleave_x(1, turned1)
+        act0 = activate(0, z0)
+
+        turned2 = gather(2)
+        z1 = first_product(quantize("x1", x_bf1, window_at[2]))
+        x_bf2 = interleave_x(2, turned2)
+        act1 = activate(1, z1)
+        gq0 = quantize("g0", apply_gain(0, act0, window_at[2] + KIB))
+
+        turned3 = gather(3)
+        z2 = first_product(quantize("x2", x_bf2, window_at[3]))
+        gq1 = quantize("g1", apply_gain(1, act1, window_at[3] + KIB))
+        wb_bf0 = interleave_wb(0, nc.scalar.copy)
+        x_bf3 = interleave_x(3, turned3, wb_raw_at[0])
+        act2 = activate(2, z2, wb_raw_at[0] + KIB)
+        wb_bf1 = interleave_wb(1, nc.vector.tensor_copy)
+        act3 = activate(3, first_product(quantize("x3", x_bf3, wb_raw_at[1])))
+        wbq = [quantize("wb0", wb_bf0, wb_raw_at[1] + KIB), quantize("wb1", wb_bf1)]
+        gq2 = quantize("g2", apply_gain(2, act2, wb_raw_at[1] + 2 * KIB))
+        gq3 = quantize("g3", apply_gain(3, act3))
+        gq = [gq0, gq1, gq2, gq3]
+
+        out_rows = out.rearrange("(a p) e -> p a e", p=P)
+
+        def second_product(name, tiles, blocks, copy):
+            width = len(blocks) * P
+            y = psum.tile([P, len(tiles), width], F32, name="y_" + name)
+            for n, a in enumerate(tiles):
+                h, column = divmod(a * P, HALF)
+                for k, b in enumerate(blocks):
+                    product(y[:, n, k * P : (k + 1) * P], wbq[h], column, gq[b])
+            staged = keep.tile([P, len(tiles), width], F32, name="staged_" + name)
+            copy(out=staged[:], in_=y[:])
+            e0 = blocks[0] * P
+            nc.sync.dma_start(out=out_rows[:, tiles[0] : tiles[-1] + 1, e0 : e0 + width], in_=staged[:])
+
+        second_product("a", [0, 1], [0, 1], nc.scalar.copy)
+        second_product("b", [2, 3], [0, 1], nc.scalar.copy)
+        second_product("c", [0, 1, 2, 3], [2], nc.vector.tensor_copy)
+        second_product("d", [0, 1], [3], nc.scalar.copy)
+        second_product("e", [2, 3], [3], nc.vector.tensor_copy)

@@ -48,19 +48,20 @@ def tile_attend_tokenmixer_kernel(tc, tok, wa, gain, wb, offs, out):
 
         nc.sync.dma_start(out=wa_raw[:], in_=wa.rearrange("(p s) f -> p s f", s=PACK))
         nc.sync.dma_start(offsets[:], offs)
-        nc.sync.dma_start(out=gain_cols[:], in_=gain.rearrange("(p t) o -> p (t o)", t=PACK))
-        for b in range(BLOCKS):
+        nc.scalar.dma_start(out=gain_cols[:], in_=gain.rearrange("(p t) o -> p (t o)", t=PACK))
+        for b in range(BLOCKS - 1):
             nc.sync.dma_start(out=windows[b][:], in_=tok[b * P : (b + 1) * P, :])
         wb_rows = wb.rearrange("(p t) j -> p t j", t=PACK)
-        for h in range(2):
-            nc.sync.dma_start(out=wb_raw[h][:], in_=wb_rows[:, :, h * HALF : (h + 1) * HALF])
+        nc.sync.dma_start(out=wb_raw[0][:], in_=wb_rows[:, :, 0:HALF])
+        nc.sync.dma_start(out=windows[BLOCKS - 1][:], in_=tok[E - P : E, :])
+        nc.sync.dma_start(out=wb_raw[1][:], in_=wb_rows[:, :, HALF:J])
 
         ident = keep.tile([P, P], F32, name="ident")
         make_identity(nc, ident[:])
         warm = keep.tile([P, 1], F32, name="warm")
         nc.scalar.activation(out=warm[:], in_=ident[:, 0:1], func=GELU)
 
-        gain_full = gain_cols[:].rearrange("p (o t) -> p o t", o=1).to_broadcast([P, P, PACK])
+        gain_row = gain_cols[:].rearrange("p (o t) -> p o t", o=1)
 
         def quantize(name, values, at=None):
             width = values.shape[1] // PACK
@@ -104,20 +105,30 @@ def tile_attend_tokenmixer_kernel(tc, tok, wa, gain, wb, offs, out):
                 product(z[:, t, :], waq, t * P, xq)
             return z
 
-        def activate(b, z, at=None):
-            act = work_tile("act%d" % b, [P, P, PACK], F32, at)
-            nc.scalar.activation(out=act[:], in_=z[:].rearrange("p t e -> p e t"), func=GELU)
-            return act
+        def activate(b, z, pieces=1):
+            width = P // pieces
+            acts = []
+            for n in range(pieces):
+                act = work_tile("act%d_%d" % (b, n), [P, width, PACK], F32)
+                cols = slice(n * width, (n + 1) * width)
+                nc.scalar.activation(out=act[:], in_=z[:].rearrange("p t e -> p e t")[:, cols, :], func=GELU)
+                acts.append(act)
+            return acts
 
-        def apply_gain(b, act, at=None):
+        def apply_gain(b, acts, at=None):
             g_bf = work_tile("g_bf%d" % b, [P, PACK * P], BF16, at)
-            nc.vector.tensor_tensor(
-                out=g_bf[:].rearrange("p (e t) -> p e t", t=PACK), in0=act[:], in1=gain_full, op=MULT
-            )
+            width = P // len(acts)
+            for n, act in enumerate(acts):
+                nc.vector.tensor_tensor(
+                    out=g_bf[:].rearrange("p (e t) -> p e t", t=PACK)[:, n * width : (n + 1) * width, :],
+                    in0=act[:],
+                    in1=gain_row.to_broadcast([P, width, PACK]),
+                    op=MULT,
+                )
             return g_bf
 
-        def interleave_wb(h, copy):
-            wb_bf = work_tile("wb_bf%d" % h, [P, PACK * HALF], BF16)
+        def interleave_wb(h, copy, at=None):
+            wb_bf = work_tile("wb_bf%d" % h, [P, PACK * HALF], BF16, at)
             copy(
                 out=wb_bf[:].rearrange("p (c i t) -> p c t i", i=PACK, t=PACK),
                 in_=wb_raw[h][:].rearrange("p t (c i) -> p c t i", i=PACK),
@@ -142,19 +153,21 @@ def tile_attend_tokenmixer_kernel(tc, tok, wa, gain, wb, offs, out):
         z1 = first_product(quantize("x1", x_bf1, window_at[2]))
         x_bf2 = interleave_x(2, turned2)
         act1 = activate(1, z1)
-        gq0 = quantize("g0", apply_gain(0, act0, window_at[2] + KIB))
+        g_bf0 = apply_gain(0, act0, window_at[2] + KIB)
+        wb_bf0 = interleave_wb(0, nc.vector.tensor_copy)
+        act2 = activate(2, first_product(quantize("x2", x_bf2, wb_raw_at[0])))
 
-        turned3 = gather(3)
-        z2 = first_product(quantize("x2", x_bf2, window_at[3]))
-        gq1 = quantize("g1", apply_gain(1, act1, window_at[3] + KIB))
-        wb_bf0 = interleave_wb(0, nc.scalar.copy)
-        x_bf3 = interleave_x(3, turned3, wb_raw_at[0])
-        act2 = activate(2, z2, wb_raw_at[0] + KIB)
-        wb_bf1 = interleave_wb(1, nc.vector.tensor_copy)
-        act3 = activate(3, first_product(quantize("x3", x_bf3, wb_raw_at[1])))
-        wbq = [quantize("wb0", wb_bf0, wb_raw_at[1] + KIB), quantize("wb1", wb_bf1)]
-        gq2 = quantize("g2", apply_gain(2, act2, wb_raw_at[1] + 2 * KIB))
-        gq3 = quantize("g3", apply_gain(3, act3))
+        x_bf3 = interleave_x(3, gather(3), window_at[0])
+        g_bf1 = apply_gain(1, act1, window_at[3])
+        gq0 = quantize("g0", g_bf0, window_at[3] + KIB)
+        wbq0 = quantize("wb0", wb_bf0, window_at[3] + 2 * KIB)
+        gq1 = quantize("g1", g_bf1)
+        act3 = activate(3, first_product(quantize("x3", x_bf3)), pieces=2)
+        g_bf2 = apply_gain(2, act2, window_at[0])
+        wb_bf1 = interleave_wb(1, nc.vector.tensor_copy, window_at[0] + KIB)
+        gq2 = quantize("g2", g_bf2, wb_raw_at[1])
+        wbq = [wbq0, quantize("wb1", wb_bf1)]
+        gq3 = quantize("g3", apply_gain(3, act3, window_at[0] + KIB))
         gq = [gq0, gq1, gq2, gq3]
 
         out_rows = out.rearrange("(a p) e -> p a e", p=P)

@@ -19,7 +19,7 @@ P = 128
 PACK = 4
 BLOCKS = E // P
 HALF = J // 2
-WA_SPLIT = 96
+WA_SPLIT = 80
 WINDOW_BYTES = 4 * T
 WB_HALF_BYTES = 4 * PACK * HALF
 KIB = 1024
@@ -135,11 +135,11 @@ def tile_attend_tokenmixer_kernel(tc, tok, wa, gain, wb, offs, out):
             )
             return wb_bf
 
-        wa_dealt = wa_raw[:].rearrange("p s (m t) -> p t m s", t=PACK)
+        wa_dealt = wa_raw[:].rearrange("p s (m t) -> p m t s", t=PACK)
         wa_bf = work_tile("wa_bf", [P, PACK * F], BF16)
-        wa_bf_dealt = wa_bf[:].rearrange("p (t m s) -> p t m s", t=PACK, s=PACK)
-        nc.vector.tensor_copy(out=wa_bf_dealt[:, :, 0:WA_SPLIT, :], in_=wa_dealt[:, :, 0:WA_SPLIT, :])
-        nc.scalar.copy(out=wa_bf_dealt[:, :, WA_SPLIT:P, :], in_=wa_dealt[:, :, WA_SPLIT:P, :])
+        wa_bf_dealt = wa_bf[:].rearrange("p (t m s) -> p m t s", t=PACK, s=PACK)
+        nc.vector.tensor_copy(out=wa_bf_dealt[:, 0:WA_SPLIT], in_=wa_dealt[:, 0:WA_SPLIT])
+        nc.scalar.copy(out=wa_bf_dealt[:, WA_SPLIT:P], in_=wa_dealt[:, WA_SPLIT:P])
         waq = quantize("wa", wa_bf)
 
         x_bf0 = interleave_x(0, gather(0))

@@ -33,7 +33,9 @@ def tile_attend_tokenmixer_kernel(tc, tok, wa, gain, wb, offs, out):
         psum = ctx.enter_context(tc.psum_pool(name="psum", bufs=1))
 
         window_at = [b * WINDOW_BYTES for b in range(BLOCKS)]
-        wb_raw_at = [BLOCKS * WINDOW_BYTES + h * WB_HALF_BYTES for h in range(2)]
+        wb_first_at = BLOCKS * WINDOW_BYTES
+        wb_third_at = wb_first_at + 6 * KIB
+        wb_fourth_at = wb_third_at + 2 * KIB
 
         def work_tile(name, shape, dtype, at=None):
             if at is None:
@@ -44,17 +46,19 @@ def tile_attend_tokenmixer_kernel(tc, tok, wa, gain, wb, offs, out):
         wa_raw = keep.tile([P, PACK, F], F32, name="wa_raw")
         gain_cols = keep.tile([P, PACK], F32, name="gain_cols")
         windows = [work_tile("window%d" % b, [P, T], F32, window_at[b]) for b in range(BLOCKS)]
-        wb_raw = [work_tile("wb_raw%d" % h, [P, PACK, HALF], F32, wb_raw_at[h]) for h in range(2)]
+        wb_first = work_tile("wb_first", [P, PACK, HALF], F32, wb_first_at)
+        wb_third = work_tile("wb_third", [P, PACK, P], F32, wb_third_at)
+        wb_fourth = work_tile("wb_fourth", [P, PACK, P], F32, wb_fourth_at)
 
         nc.sync.dma_start(out=wa_raw[:], in_=wa.rearrange("(p s) f -> p s f", s=PACK))
         nc.sync.dma_start(offsets[:], offs)
         nc.scalar.dma_start(out=gain_cols[:], in_=gain.rearrange("(p t) o -> p (t o)", t=PACK))
-        for b in range(BLOCKS - 1):
+        for b in range(BLOCKS):
             nc.sync.dma_start(out=windows[b][:], in_=tok[b * P : (b + 1) * P, :])
         wb_rows = wb.rearrange("(p t) j -> p t j", t=PACK)
-        nc.sync.dma_start(out=wb_raw[0][:], in_=wb_rows[:, :, 0:HALF])
-        nc.sync.dma_start(out=windows[BLOCKS - 1][:], in_=tok[E - P : E, :])
-        nc.sync.dma_start(out=wb_raw[1][:], in_=wb_rows[:, :, HALF:J])
+        nc.sync.dma_start(out=wb_first[:], in_=wb_rows[:, :, 0:HALF])
+        nc.sync.dma_start(out=wb_third[:], in_=wb_rows[:, :, HALF : HALF + P])
+        nc.sync.dma_start(out=wb_fourth[:], in_=wb_rows[:, :, HALF + P : J])
 
         ident = keep.tile([P, P], F32, name="ident")
         make_identity(nc, ident[:])
@@ -105,11 +109,11 @@ def tile_attend_tokenmixer_kernel(tc, tok, wa, gain, wb, offs, out):
                 product(z[:, t, :], waq, t * P, xq)
             return z
 
-        def activate(b, z, pieces=1):
+        def activate(b, z, pieces=1, at=None):
             width = P // pieces
             acts = []
             for n in range(pieces):
-                act = work_tile("act%d_%d" % (b, n), [P, width, PACK], F32)
+                act = work_tile("act%d_%d" % (b, n), [P, width, PACK], F32, at if n == 0 else None)
                 cols = slice(n * width, (n + 1) * width)
                 nc.scalar.activation(out=act[:], in_=z[:].rearrange("p t e -> p e t")[:, cols, :], func=GELU)
                 acts.append(act)
@@ -127,12 +131,14 @@ def tile_attend_tokenmixer_kernel(tc, tok, wa, gain, wb, offs, out):
                 )
             return g_bf
 
-        def interleave_wb(h, copy, at=None):
+        def interleave_wb(h, sources, at=None):
             wb_bf = work_tile("wb_bf%d" % h, [P, PACK * HALF], BF16, at)
-            copy(
-                out=wb_bf[:].rearrange("p (c i t) -> p c t i", i=PACK, t=PACK),
-                in_=wb_raw[h][:].rearrange("p t (c i) -> p c t i", i=PACK),
-            )
+            for n, (copy, raw) in enumerate(sources):
+                share = wb_bf[:, n * PACK * P : (n + 1) * PACK * P]
+                copy(
+                    out=share.rearrange("p (c i t) -> p c t i", i=PACK, t=PACK),
+                    in_=raw.rearrange("p t (c i) -> p c t i", i=PACK),
+                )
             return wb_bf
 
         wa_dealt = wa_raw[:].rearrange("p s (m t) -> p m t s", t=PACK)
@@ -154,38 +160,41 @@ def tile_attend_tokenmixer_kernel(tc, tok, wa, gain, wb, offs, out):
         x_bf2 = interleave_x(2, turned2)
         act1 = activate(1, z1)
         g_bf0 = apply_gain(0, act0, window_at[2] + KIB)
-        wb_bf0 = interleave_wb(0, nc.vector.tensor_copy)
-        act2 = activate(2, first_product(quantize("x2", x_bf2, wb_raw_at[0])))
 
-        x_bf3 = interleave_x(3, gather(3), window_at[0])
-        g_bf1 = apply_gain(1, act1, window_at[3])
+        turned3 = gather(3)
+        z2 = first_product(quantize("x2", x_bf2, window_at[3]))
         gq0 = quantize("g0", g_bf0, window_at[3] + KIB)
-        wbq0 = quantize("wb0", wb_bf0, window_at[3] + 2 * KIB)
-        gq1 = quantize("g1", g_bf1)
-        act3 = activate(3, first_product(quantize("x3", x_bf3)), pieces=2)
-        g_bf2 = apply_gain(2, act2, window_at[0])
-        wb_bf1 = interleave_wb(1, nc.vector.tensor_copy, window_at[0] + KIB)
-        gq2 = quantize("g2", g_bf2, wb_raw_at[1])
+        wb_bf0 = interleave_wb(0, [(nc.scalar.copy, wb_first[:, :, 0:P]), (nc.vector.tensor_copy, wb_first[:, :, P:HALF])])
+        g_bf1 = apply_gain(1, act1, wb_first_at)
+        x_bf3 = interleave_x(3, turned3, wb_first_at + 7 * KIB // 2)
+        act2 = activate(2, z2, at=wb_first_at + KIB)
+        z3 = first_product(quantize("x3", x_bf3))
+        wbq0 = quantize("wb0", wb_bf0, wb_first_at + 4 * KIB)
+        gq1 = quantize("g1", g_bf1, wb_first_at + 7 * KIB // 2)
+        wb_bf1 = interleave_wb(1, [(nc.vector.tensor_copy, wb_third[:]), (nc.scalar.copy, wb_fourth[:])], window_at[0])
+        act3 = activate(3, z3, pieces=2, at=wb_fourth_at)
+        g_bf2 = apply_gain(2, act2, wb_third_at)
         wbq = [wbq0, quantize("wb1", wb_bf1)]
-        gq3 = quantize("g3", apply_gain(3, act3, window_at[0] + KIB))
+        gq2 = quantize("g2", g_bf2)
+        gq3 = quantize("g3", apply_gain(3, act3, window_at[0]))
         gq = [gq0, gq1, gq2, gq3]
 
         out_rows = out.rearrange("(a p) e -> p a e", p=P)
 
-        def second_product(name, tiles, blocks, copy):
+        def second_product(name, tiles, blocks, copy, at=None):
             width = len(blocks) * P
             y = psum.tile([P, len(tiles), width], F32, name="y_" + name)
             for n, a in enumerate(tiles):
                 h, column = divmod(a * P, HALF)
                 for k, b in enumerate(blocks):
                     product(y[:, n, k * P : (k + 1) * P], wbq[h], column, gq[b])
-            staged = keep.tile([P, len(tiles), width], F32, name="staged_" + name)
+            staged = work_tile("staged_" + name, [P, len(tiles), width], F32, at)
             copy(out=staged[:], in_=y[:])
             e0 = blocks[0] * P
             nc.sync.dma_start(out=out_rows[:, tiles[0] : tiles[-1] + 1, e0 : e0 + width], in_=staged[:])
 
-        second_product("a", [0, 1], [0, 1], nc.scalar.copy)
+        second_product("a", [0, 1], [0, 1], nc.scalar.copy, wb_fourth_at + KIB)
         second_product("b", [2, 3], [0, 1], nc.scalar.copy)
-        second_product("c", [0, 1, 2, 3], [2], nc.vector.tensor_copy)
+        second_product("c", [0, 1, 2, 3], [2], nc.vector.tensor_copy, window_at[0])
         second_product("d", [0, 1], [3], nc.scalar.copy)
         second_product("e", [2, 3], [3], nc.vector.tensor_copy)

from contextlib import ExitStack

import concourse.mybir as mybir
from concourse.masks import make_identity

E, T, I, F, J = 512, 2048, 512, 512, 512
FLOPS = 2 * I * F * E + 2 * F * J * E

F32 = mybir.dt.float32
BF16 = mybir.dt.bfloat16
U32 = mybir.dt.uint32
U16 = mybir.dt.uint16
U8 = mybir.dt.uint8
FP8X4 = mybir.dt.float8_e4m3fn_x4
GELU = mybir.ActivationFunctionType.Gelu_apprx_tanh
MULT = mybir.AluOpType.mult

P = 128
PACK = 4
BLOCKS = E // P
HALF = J // 2
WA_SPLIT = 80
WINDOW_BYTES = 4 * T
WB_HALF_BYTES = 4 * PACK * HALF
KIB = 1024


def tile_attend_tokenmixer_kernel(tc, tok, wa, gain, wb, offs, out):
    nc = tc.nc
    with ExitStack() as ctx:
        keep = ctx.enter_context(tc.tile_pool(name="keep", bufs=1))
        arena = ctx.enter_context(tc.tile_pool(name="arena", bufs=1))
        psum = ctx.enter_context(tc.psum_pool(name="psum", bufs=1))

        window_at = [b * WINDOW_BYTES for b in range(BLOCKS)]
        wb_first_at = BLOCKS * WINDOW_BYTES
        wb_third_at = wb_first_at + 6 * KIB
        wb_fourth_at = wb_third_at + 2 * KIB

        def work_tile(name, shape, dtype, at=None):
            if at is None:
                return keep.tile(shape, dtype, name=name, align_bytes=64)
            return arena.tile(shape, dtype, name=name, align_bytes=64, offset=at)

        offsets = keep.tile([P, I // 16], U16, name="offsets")
        wa_raw = keep.tile([P, PACK, F], F32, name="wa_raw")
        gain_cols = keep.tile([P, PACK], F32, name="gain_cols")
        windows = [work_tile("window%d" % b, [P, T], F32, window_at[b]) for b in range(BLOCKS)]
        wb_first = work_tile("wb_first", [P, PACK, HALF], F32, wb_first_at)
        wb_third = work_tile("wb_third", [P, PACK, P], F32, wb_third_at)
        wb_fourth = work_tile("wb_fourth", [P, PACK, P], F32, wb_fourth_at)

        nc.sync.dma_start(out=wa_raw[:], in_=wa.rearrange("(p s) f -> p s f", s=PACK))
        nc.sync.dma_start(offsets[:], offs)
        nc.scalar.dma_start(out=gain_cols[:], in_=gain.rearrange("(p t) o -> p (t o)", t=PACK))
        for b in range(BLOCKS):
            nc.sync.dma_start(out=windows[b][:], in_=tok[b * P : (b + 1) * P, :])
        wb_rows = wb.rearrange("(p t) j -> p t j", t=PACK)
        nc.sync.dma_start(out=wb_first[:], in_=wb_rows[:, :, 0:HALF])
        nc.sync.dma_start(out=wb_third[:], in_=wb_rows[:, :, HALF : HALF + P])
        nc.sync.dma_start(out=wb_fourth[:], in_=wb_rows[:, :, HALF + P : J])

        ident = keep.tile([P, P], F32, name="ident")
        make_identity(nc, ident[:])
        warm = keep.tile([P, 1], F32, name="warm")
        nc.scalar.activation(out=warm[:], in_=ident[:, 0:1], func=GELU)

        gain_row = gain_cols[:].rearrange("p (o t) -> p o t", o=1)

        def quantize(name, values, at=None):
            width = values.shape[1] // PACK
            codes = work_tile(name + "_codes", [P, width], U32, at)
            scales = work_tile(name + "_scales", [P, width], U8)
            nc.vector.quantize_mx(out=codes[:].bitcast(FP8X4), scales=scales[:], in_=values[:])
            return codes, scales

        def product(dst, stationary, column, moving):
            cols = slice(column, column + P)
            nc.tensor.matmul_mx(
                out=dst,
                lhsT=stationary[0][:, cols].bitcast(FP8X4),
                lhsT_scale=stationary[1][:, cols],
                rhs=moving[0][:].bitcast(FP8X4),
                rhs_scale=moving[1][:],
                start=True,
                stop=True,
            )

        def gather(b):
            picked = work_tile("picked%d" % b, [P, I], BF16)
            nc.vector.tensor_copy(picked[:], windows[b][:].indirect(offsets[:]))
            words = picked[:].bitcast(F32)
            turned = psum.tile([P, 2, P], F32, name="turned", tag="turned")
            for u in range(2):
                nc.tensor.transpose(turned[:, u, :], words[:, u : I // 2 : 2], ident[:])
            return turned

        def interleave_x(b, turned, at=None):
            x_bf = work_tile("x_bf%d" % b, [P, PACK * P], BF16, at)
            nc.scalar.copy(
                out=x_bf[:].bitcast(F32).rearrange("p (e u) -> p e u", u=2),
                in_=turned[:].rearrange("p u e -> p e u"),
            )
            return x_bf

        def first_product(xq):
            z = psum.tile([P, PACK, P], F32, name="z", bufs=2)
            for t in range(PACK):
                product(z[:, t, :], waq, t * P, xq)
            return z

        def activate(b, z, pieces=1, at=None):
            width = P // pieces
            acts = []
            for n in range(pieces):
                act = work_tile("act%d_%d" % (b, n), [P, width, PACK], F32, at if n == 0 else None)
                cols = slice(n * width, (n + 1) * width)
                nc.scalar.activation(out=act[:], in_=z[:].rearrange("p t e -> p e t")[:, cols, :], func=GELU)
                acts.append(act)
            return acts

        def apply_gain(b, acts, at=None):
            g_bf = work_tile("g_bf%d" % b, [P, PACK * P], BF16, at)
            width = P // len(acts)
            for n, act in enumerate(acts):
                nc.vector.tensor_tensor(
                    out=g_bf[:].rearrange("p (e t) -> p e t", t=PACK)[:, n * width : (n + 1) * width, :],
                    in0=act[:],
                    in1=gain_row.to_broadcast([P, width, PACK]),
                    op=MULT,
                )
            return g_bf

        def interleave_wb(h, sources, at=None):
            wb_bf = work_tile("wb_bf%d" % h, [P, PACK * HALF], BF16, at)
            for n, (copy, raw) in enumerate(sources):
                share = wb_bf[:, n * PACK * P : (n + 1) * PACK * P]
                copy(
                    out=share.rearrange("p (c i t) -> p c t i", i=PACK, t=PACK),
                    in_=raw.rearrange("p t (c i) -> p c t i", i=PACK),
                )
            return wb_bf

        wa_dealt = wa_raw[:].rearrange("p s (m t) -> p m t s", t=PACK)
        wa_bf = work_tile("wa_bf", [P, PACK * F], BF16)
        wa_bf_dealt = wa_bf[:].rearrange("p (t m s) -> p m t s", t=PACK, s=PACK)
        nc.vector.tensor_copy(out=wa_bf_dealt[:, 0:WA_SPLIT], in_=wa_dealt[:, 0:WA_SPLIT])
        nc.scalar.copy(out=wa_bf_dealt[:, WA_SPLIT:P], in_=wa_dealt[:, WA_SPLIT:P])
        waq = quantize("wa", wa_bf)

        x_bf0 = interleave_x(0, gather(0))

        turned1 = gather(1)
        z0 = first_product(quantize("x0", x_bf0, window_at[1]))
        x_bf1 = interleave_x(1, turned1)
        act0 = activate(0, z0)

        turned2 = gather(2)
        z1 = first_product(quantize("x1", x_bf1, window_at[2]))
        x_bf2 = interleave_x(2, turned2)
        act1 = activate(1, z1)
        g_bf0 = apply_gain(0, act0, window_at[2] + KIB)

        turned3 = gather(3)
        z2 = first_product(quantize("x2", x_bf2, window_at[3]))
        gq0 = quantize("g0", g_bf0, window_at[3] + KIB)
        wb_bf0 = interleave_wb(0, [(nc.scalar.copy, wb_first[:, :, 0:P]), (nc.vector.tensor_copy, wb_first[:, :, P:HALF])])
        g_bf1 = apply_gain(1, act1, wb_first_at)
        x_bf3 = interleave_x(3, turned3, wb_first_at + 7 * KIB // 2)
        act2 = activate(2, z2, at=wb_first_at + KIB)
        z3 = first_product(quantize("x3", x_bf3))
        wbq0 = quantize("wb0", wb_bf0, wb_first_at + 4 * KIB)
        gq1 = quantize("g1", g_bf1, wb_first_at + 7 * KIB // 2)
        wb_bf1 = interleave_wb(1, [(nc.vector.tensor_copy, wb_third[:]), (nc.scalar.copy, wb_fourth[:])], window_at[0])
        act3 = activate(3, z3, pieces=2, at=wb_fourth_at)
        g_bf2 = apply_gain(2, act2, wb_third_at)
        wbq = [wbq0, quantize("wb1", wb_bf1)]
        gq2 = quantize("g2", g_bf2)
        gq3 = quantize("g3", apply_gain(3, act3, window_at[0]))
        gq = [gq0, gq1, gq2, gq3]

        out_rows = out.rearrange("(a p) e -> p a e", p=P)

        def second_product(name, tiles, blocks, copy, at=None):
            width = len(blocks) * P
            y = psum.tile([P, len(tiles), width], F32, name="y_" + name)
            for n, a in enumerate(tiles):
                h, column = divmod(a * P, HALF)
                for k, b in enumerate(blocks):
                    product(y[:, n, k * P : (k + 1) * P], wbq[h], column, gq[b])
            staged = work_tile("staged_" + name, [P, len(tiles), width], F32, at)
            copy(out=staged[:], in_=y[:])
            e0 = blocks[0] * P
            nc.sync.dma_start(out=out_rows[:, tiles[0] : tiles[-1] + 1, e0 : e0 + width], in_=staged[:])

        second_product("a", [0, 1], [0, 1], nc.scalar.copy, wb_fourth_at + KIB)
        second_product("b", [2, 3], [0, 1], nc.scalar.copy)
        second_product("c", [0, 1, 2, 3], [2], nc.vector.tensor_copy, window_at[0])
        second_product("d", [0, 1], [3], nc.scalar.copy)
        second_product("e", [2, 3], [3], nc.vector.tensor_copy)
